import numpy as np
import ml_dtypes


def mxq(x, axis, fmt="e4m3"):
    dtype, down = {"e4m3": (ml_dtypes.float8_e4m3fn, 7), "e5m2": (ml_dtypes.float8_e5m2, 14)}[fmt]
    v = np.moveaxis(np.asarray(x, np.float32).astype(ml_dtypes.bfloat16).astype(np.float64), axis, -1)
    blocks = v.reshape(v.shape[:-1] + (-1, 32))
    amax = np.abs(blocks).max(-1, keepdims=True)
    byte = np.maximum(np.where(amax > 0, np.frexp(amax)[1] - 1 + 127, 0) - down, 1)
    scale = np.exp2(byte - 127.0)
    codes = (blocks / scale).astype(np.float32).astype(dtype).astype(np.float64)
    return np.moveaxis((codes * scale).reshape(v.shape), -1, axis)


WIDE = False


def mx_kscale(k):
    if not WIDE:
        return np.ones(k)
    levels = np.array([30, -30])
    if k % 512:
        return np.exp2(np.random.permutation(np.resize(levels, k // 32))).repeat(32)
    a = np.empty((k // 512, 16))
    for p in range(k // 512):
        a[p, :8] = np.random.permutation(np.resize(levels, 8))
        for g in range(8):
            far = levels[np.abs(levels - a[p, g]) >= 10]
            a[p, g + 8] = far[np.random.randint(len(far))]
    return np.exp2(a.ravel()).repeat(32)


def f64(x):
    return np.asarray(x).astype(np.float64)


def striped(idx):
    return np.tile(np.asarray(idx).reshape(-1, 16).T, (8, 1)).astype(np.uint16)


def unstriped(offs):
    return offs[:16].T.reshape(-1).astype(np.int64)


E2M1 = np.array([0.0, 0.5, 1.0, 1.5, 2.0, 3.0, 4.0, 6.0, -0.0, -0.5, -1.0, -1.5, -2.0, -3.0, -4.0, -6.0])


def pack_weight(w, fmt):
    k, n = w.shape
    w = f64(np.asarray(w, np.float32).astype(ml_dtypes.bfloat16)).reshape(k // 32, 32, n)
    amax = np.abs(w).max(1)
    if fmt in ("e4m3", "e5m2"):
        byte = np.frexp(amax)[1] - 1 + 127 - (7 if fmt == "e4m3" else 14)
    else:
        mant, ex = np.frexp(amax / 6.0)
        byte = np.where(mant > 0.5, ex, ex - 1) + 127
    byte = np.clip(np.where(amax > 0, byte, 1), 1, 254)
    scaled = (w * np.exp2(127.0 - byte)[:, None, :]).reshape(k, n).astype(np.float32)
    by_word = np.ascontiguousarray(scaled.reshape(k // 512, 128, 4, n).transpose(0, 1, 3, 2))
    if fmt in ("e4m3", "e5m2"):
        words = by_word.astype(ml_dtypes.float8_e4m3fn if fmt == "e4m3" else ml_dtypes.float8_e5m2).view(np.uint8)
    else:
        c = by_word.astype(ml_dtypes.float4_e2m1fn).view(np.uint8) & 0xF
        words = (c[..., 0::2] | (c[..., 1::2] << 4)).reshape(k // 512, 128, 2 * n)
    return np.ascontiguousarray(words), np.ascontiguousarray(byte.astype(np.uint8).reshape(k // 512, 16, n))


def unpack_weight(words, scales, fmt):
    g, _, n = scales.shape
    words = np.ascontiguousarray(words).reshape(g, 128, n, -1)
    if fmt in ("e4m3", "e5m2"):
        vals = words.view(ml_dtypes.float8_e4m3fn if fmt == "e4m3" else ml_dtypes.float8_e5m2).astype(np.float64)
    else:
        nib = np.empty((g, 128, n, 4), np.uint8)
        nib[..., 0::2] = words & 0xF
        nib[..., 1::2] = words >> 4
        vals = E2M1[nib]
    vals = vals * np.repeat(np.exp2(scales.astype(np.float64) - 127.0), 8, axis=1)[..., None]
    return vals.transpose(0, 1, 3, 2).reshape(g * 512, n)


K, T, J, R, F, Z, O, U, D, N, E = 512, 1024, 256, 512, 512, 1024, 128, 128, 256, 256, 512


def setup_inputs():
    n = np.random.standard_normal
    idx = np.random.permutation(T)[:J]
    idx2 = np.random.permutation(Z)[:J]
    idx3 = np.random.permutation(J)[:O]
    idx4 = np.random.permutation(J)[:U]
    idx5 = np.random.permutation(T)[:D]
    idx6 = np.random.permutation(E)[:D]
    idx7 = np.random.permutation(E)[:D]
    fk = mx_kscale(K)
    ff = mx_kscale(F)
    fr = mx_kscale(R)
    xtp = pack_weight(n((K, T)) / fk[:, None], "e4m3")
    xop = pack_weight(n((F, Z)) / ff[:, None], "e2m1")
    wp = pack_weight(n((K, R)) * 1 / np.sqrt(K) * fk[:, None] * fr, "e2m1")
    w2p = pack_weight(n((K, R)) * 1 / np.sqrt(K) * fk[:, None], "e5m2")
    w0p = pack_weight(n((F, R)) * 1 / np.sqrt(F) * ff[:, None], "e5m2")
    wbp = pack_weight(n((R, N)) * 1 / np.sqrt(R) / fr[:, None], "e5m2")
    wsp = pack_weight(n((K, N)) * 1 / np.sqrt(K) * fk[:, None], "e5m2")
    return {
        "xt_words": xtp[0],
        "xt_scales": xtp[1],
        "xo_words": xop[0],
        "xo_scales": xop[1],
        "w_words": wp[0],
        "w_scales": wp[1],
        "w2_words": w2p[0],
        "w2_scales": w2p[1],
        "w0_words": w0p[0],
        "w0_scales": w0p[1],
        "wb_words": wbp[0],
        "wb_scales": wbp[1],
        "ws_words": wsp[0],
        "ws_scales": wsp[1],
        "offs": striped(idx),
        "offs2": striped(idx2),
        "offs3": striped(idx3),
        "offs4": striped(idx4),
        "offs5": striped(idx5),
        "offs6": striped(idx6),
        "offs7": striped(idx7),
    }


def reference(xt_words, xt_scales, xo_words, xo_scales, w_words, w_scales, w2_words, w2_scales, w0_words, w0_scales, wb_words, wb_scales, ws_words, ws_scales, offs, offs2, offs3, offs4, offs5, offs6, offs7):
    idx = unstriped(offs)
    idx2 = unstriped(offs2)
    idx3 = unstriped(offs3)
    idx4 = unstriped(offs4)
    idx5 = unstriped(offs5)
    idx6 = unstriped(offs6)
    idx7 = unstriped(offs7)
    xtu = unpack_weight(xt_words, xt_scales, "e4m3")
    xou = unpack_weight(xo_words, xo_scales, "e2m1")
    wu = unpack_weight(w_words, w_scales, "e2m1")
    w2u = unpack_weight(w2_words, w2_scales, "e5m2")
    w0u = unpack_weight(w0_words, w0_scales, "e5m2")
    wbu = unpack_weight(wb_words, wb_scales, "e5m2")
    wsu = unpack_weight(ws_words, ws_scales, "e5m2")
    xtidxg = xtu[:, idx]
    a = wu.T @ xtidxg
    xoidx2g = xou[:, idx2]
    b = w2u.T @ xtidxg + w0u.T @ xoidx2g
    lb = b[:, 0:1]
    la = a[:, 0:1]
    h1 = a[:, idx3] * lb
    h2 = b[:, idx4] * la
    hid = np.concatenate([h1, h2], axis=1)
    hidq = mxq(hid, 0, "e4m3")
    xtidx5g = xtu[:, idx5]
    p = wbu.T @ hidq + wsu.T @ xtidx5g
    pa = np.zeros((N, E))
    pa[:, idx6] = p
    pb = np.zeros((N, E))
    pb[:, idx7] = p
    y = pa + pb
    return y

@@ -1,0 +1,229 @@
+from contextlib import ExitStack
+
+import concourse.mybir as mybir
+
+K, T, J, R, F, Z, O, U, D, N, E = 512, 1024, 256, 512, 512, 1024, 128, 128, 256, 256, 512
+FLOPS = 2 * (K * R * J + K * R * J + F * R * J + R * N * D + K * N * D)
+
+F32 = mybir.dt.float32
+BF16 = mybir.dt.bfloat16
+I32 = mybir.dt.int32
+U32 = mybir.dt.uint32
+U16 = mybir.dt.uint16
+U8 = mybir.dt.uint8
+E4M3 = mybir.dt.float8_e4m3fn_x4
+E5M2 = mybir.dt.float8_e5m2_x4
+E2M1 = mybir.dt.float4_e2m1fn_x4
+COPY = mybir.ActivationFunctionType.Copy
+ADD = mybir.AluOpType.add
+
+P = 128
+PACK = 4
+QUADS = 4
+QROWS = 4
+HALF = D // 2
+LINE = 16
+
+
+def dealt(dst, src, run):
+    return (dst.rearrange("p (t c i) -> p c t i", t=PACK, i=run),
+            src.rearrange("p (c i t) -> p c t i", t=PACK, i=run))
+
+
+def tile_list_sidebyside_leaned_further_pagetwice_kernel(
+        tc, xt_words, xt_scales, xo_words, xo_scales, w_words, w_scales, w2_words, w2_scales, w0_words, w0_scales,
+        wb_words, wb_scales, ws_words, ws_scales, offs, offs2, offs3, offs4, offs5, offs6, offs7, out):
+    nc = tc.nc
+    with ExitStack() as ctx:
+        sb = ctx.enter_context(tc.tile_pool(name="sb", bufs=1))
+        psum = ctx.enter_context(tc.psum_pool(name="psum", bufs=1))
+
+        def tile(name, shape, dtype, tag=None):
+            return sb.tile(shape, dtype, name=name, tag=tag or name, align_bytes=64)
+
+        def load_list(name, src):
+            lst = sb.tile(list(src.shape), U16, name=name)
+            nc.sync.dma_start(lst[:], src)
+            return lst
+
+        def load_words(queue, name, src, dtype, cols):
+            words = tile(name, [P, cols], dtype)
+            queue.dma_start(words[:].bitcast(I32), src.bitcast(I32))
+            return words
+
+        def fp8_rows(src):
+            return src[0].rearrange("p n t -> p (n t)")
+
+        def zeroed_plane(name, cols):
+            plane = tile(name, [P, cols], U8)
+            nc.vector.memset(plane[:].bitcast(I32), 0)
+            return plane
+
+        def load_plane(plane, src):
+            rows = src[0].bitcast(I32)
+            for q in range(QUADS):
+                nc.sync.dma_start(plane[32 * q:32 * q + QROWS, :].bitcast(I32), rows[QROWS * q:QROWS * (q + 1), :])
+
+        def zeroed_fold(name, cols):
+            fold = tile(name, [P, QUADS, cols // 4], I32)
+            nc.vector.memset(fold[0:64, 0:QUADS:2, :], 0)
+            return fold
+
+        def load_fold(queue, fold, slot, src):
+            cols = src.shape[2] // 4
+            queue.dma_start(fold[0:QROWS, :, slot * cols:(slot + 1) * cols],
+                            src[0].bitcast(I32).rearrange("(q r) c -> r q c", r=QROWS))
+
+        def load_pair(pair, slot, src):
+            cols = src.shape[2] // 4
+            rows = src[0].bitcast(I32).rearrange("(high odd r) c -> odd r high c", odd=2, r=QROWS)
+            for odd in range(2):
+                nc.sync.dma_start(pair[32 * odd:32 * odd + QROWS, :, slot * cols:(slot + 1) * cols], rows[odd])
+
+        def unfold(fold):
+            nc.vector.tensor_copy(fold[32:32 + QROWS, 0:3, :], fold[0:QROWS, 1:4, :])
+            nc.vector.tensor_copy(fold[64:128, 0, :], fold[0:64, 2, :])
+            return fold[:, 0, :].bitcast(U8)
+
+        def gather(name, window, entries, dtype, tag=None):
+            picked = tile(name, [P, 16 * entries.shape[1]], dtype, tag)
+            nc.vector.tensor_copy(picked[:], window[:].indirect(entries))
+            return picked
+
+        xt_plane = zeroed_plane("xt_plane", T)
+        w_fold = zeroed_fold("w_fold", R)
+        w20_pair = tile("w20_pair", [P, 2, 2 * R // 4], I32)
+        nc.vector.memset(w20_pair[0:64], 0)
+        xo_plane = zeroed_plane("xo_plane", Z)
+        ws_plane = zeroed_plane("ws_plane", N)
+        wb_plane = zeroed_plane("wb_plane", N)
+
+        idx = load_list("idx", offs)
+        w_raw = load_words(nc.scalar, "w_raw", w_words[0], U16, R)
+        xt_tab = load_words(nc.sync, "xt_tab", fp8_rows(xt_words), U32, T)
+        load_fold(nc.scalar, w_fold, 0, w_scales)
+        load_plane(xt_plane, xt_scales)
+        w2_raw = load_words(nc.sync, "w2_raw", fp8_rows(w2_words), U32, R)
+        load_pair(w20_pair, 0, w2_scales)
+        load_pair(w20_pair, 1, w0_scales)
+        idx2 = load_list("idx2", offs2)
+        xo_tab = load_words(nc.sync, "xo_tab", xo_words[0], U16, Z)
+        w0_raw = load_words(nc.sync, "w0_raw", fp8_rows(w0_words), U32, R)
+        load_plane(xo_plane, xo_scales)
+        idx5 = load_list("idx5", offs5)
+        idx3 = load_list("idx3", offs3)
+        idx4 = load_list("idx4", offs4)
+        ws_codes = load_words(nc.sync, "ws_codes", fp8_rows(ws_words), U32, N)
+        load_plane(ws_plane, ws_scales)
+        wb_codes = load_words(nc.sync, "wb_codes", fp8_rows(wb_words), U32, N)
+        load_plane(wb_plane, wb_scales)
+        idx6 = load_list("idx6", offs6)
+        idx7 = load_list("idx7", offs7)
+
+        w_codes = tile("w_codes", [P, R], U16)
+        nc.scalar.copy(*dealt(w_codes[:], w_raw[:], LINE // 2))
+        w2_codes = tile("w2_codes", [P, R], U32)
+        nc.scalar.copy(*dealt(w2_codes[:], w2_raw[:], LINE // 4))
+        w0_codes = tile("w0_codes", [P, R], U32)
+        nc.scalar.copy(*dealt(w0_codes[:], w0_raw[:], LINE // 4))
+
+        xg_scale = gather("xg_scale", xt_plane, idx[:], U8)
+        w_plane = unfold(w_fold)
+        w_scale = tile("w_scale", [P, R], U8)
+        nc.vector.tensor_copy(*dealt(w_scale[:], w_plane, LINE))
+        xg_codes = gather("xg_codes", xt_tab, idx[:], U32)
+        nc.vector.tensor_copy(w20_pair[64:128, 0, :], w20_pair[0:64, 1, :])
+        w20_plane = w20_pair[:, 0, :].bitcast(U8)
+        w2_scale = tile("w2_scale", [P, R], U8)
+        nc.vector.tensor_copy(*dealt(w2_scale[:], w20_plane[:, 0:R], LINE))
+        w0_scale = tile("w0_scale", [P, R], U8)
+        nc.vector.tensor_copy(*dealt(w0_scale[:], w20_plane[:, R:2 * R], LINE))
+        og_codes = gather("og_codes", xo_tab, idx2[:], U16)
+        og_scale = gather("og_scale", xo_plane, idx2[:], U8)
+
+        pages = {}
+        for (half, which), tag in zip(((0, 0), (0, 1), (1, 0), (1, 1)), ("w_raw", "w2_raw", "w0_raw", "xo_tab")):
+            pages[half, which] = tile(f"page{half}{which}", [P, E], F32, tag)
+            nc.gpsimd.memset(pages[half, which][:], 0.0)
+
+        a_rows, b_rows, b_acc = [], [], []
+        for t in range(PACK):
+            cols = slice(t * P, (t + 1) * P)
+            acc = psum.tile([P, J], F32, name=f"a_acc{t}", tag=f"bank{t}")
+            nc.tensor.matmul_mx(acc[:], lhsT=w_codes[:, cols].bitcast(E2M1), lhsT_scale=w_scale[:, cols],
+                                rhs=xg_codes[:].bitcast(E4M3), rhs_scale=xg_scale[:], start=True, stop=True)
+            a_rows.append(tile(f"a_rows{t}", [P, J], F32))
+            nc.scalar.copy(a_rows[t][:], acc[:])
+        for t in range(PACK):
+            cols = slice(t * P, (t + 1) * P)
+            b_acc.append(psum.tile([P, J], F32, name=f"b_acc{t}", tag=f"bank{PACK + t}"))
+            nc.tensor.matmul_mx(b_acc[t][:], lhsT=w2_codes[:, cols].bitcast(E5M2), lhsT_scale=w2_scale[:, cols],
+                                rhs=xg_codes[:].bitcast(E4M3), rhs_scale=xg_scale[:], start=True, stop=False)
+        for t in range(PACK):
+            cols = slice(t * P, (t + 1) * P)
+            nc.tensor.matmul_mx(b_acc[t][:], lhsT=w0_codes[:, cols].bitcast(E5M2), lhsT_scale=w0_scale[:, cols],
+                                rhs=og_codes[:].bitcast(E2M1), rhs_scale=og_scale[:], start=False, stop=True)
+            b_rows.append(tile(f"b_rows{t}", [P, J], F32))
+            nc.vector.tensor_copy(b_rows[t][:], b_acc[t][:])
+
+
+        p_acc = {}
+
+        def short_way(part, scale_tag, codes_tag):
+            entries = idx5[:, part * HALF // 16:(part + 1) * HALF // 16]
+            sg_scale = gather(f"sg_scale{part}", xt_plane, entries, U8, scale_tag)
+            sg_codes = gather(f"sg_codes{part}", xt_tab, entries, U32, codes_tag)
+            p_acc[part] = psum.tile([P, 2, HALF], F32, name=f"p_acc{part}", tag=f"bank{part}")
+            for half in range(2):
+                cols = slice(half * P, (half + 1) * P)
+                nc.tensor.matmul_mx(p_acc[part][:, half, :], lhsT=ws_codes[:, cols].bitcast(E5M2), lhsT_scale=ws_plane[:, cols],
+                                    rhs=sg_codes[:].bitcast(E4M3), rhs_scale=sg_scale[:], start=half == 0, stop=False)
+
+        def lean(part, rows, lst, scales, tag):
+            hid = tile(f"hid{part}", [P, PACK, HALF], BF16, tag)
+            for t in range(PACK):
+                nc.scalar.activation(hid[:, t, :], rows[t][:].indirect(lst[:]), COPY, scale=scales[t])
+            return hid
+
+        def quantise(part, hid):
+            woven = tile(f"woven{part}", [P, HALF, PACK], BF16, "woven")
+            nc.vector.tensor_copy(woven[:].rearrange("p (c i) t -> p c t i", i=4),
+                                  hid[:].rearrange("p t (c i) -> p c t i", i=4))
+            hid_codes = tile(f"hid_codes{part}", [P, HALF], U32)
+            hid_scale = tile(f"hid_scale{part}", [P, HALF], U8)
+            nc.vector.quantize_mx(hid_codes[:].bitcast(E4M3), hid_scale[:], woven[:].rearrange("p d t -> p (d t)"))
+            return hid_codes, hid_scale
+
+        def product(part, hid_codes, hid_scale):
+            for half in range(2):
+                cols = slice(half * P, (half + 1) * P)
+                nc.tensor.matmul_mx(p_acc[part][:, half, :], lhsT=wb_codes[:, cols].bitcast(E5M2), lhsT_scale=wb_plane[:, cols],
+                                    rhs=hid_codes[:].bitcast(E4M3), rhs_scale=hid_scale[:], start=False, stop=half == 1)
+            p_rows = tile(f"p_rows{part}", [P, 2, HALF], F32)
+            nc.vector.tensor_copy(p_rows[:], p_acc[part][:])
+            return p_rows
+
+        def scatter(part, p_rows):
+            entries = slice(part * HALF // 16, (part + 1) * HALF // 16)
+            for half in range(2):
+                nc.vector.tensor_copy(pages[half, 0][:].indirect(idx6[:, entries]), p_rows[:, half, :])
+                nc.scalar.activation(pages[half, 1][:].indirect(idx7[:, entries]), p_rows[:, half, :], COPY)
+
+        short_way(0, "og_scale", "og_codes")
+        la_last = tile("la_last", [P, 1], F32)
+        nc.scalar.copy(la_last[:], a_rows[PACK - 1][:, 0:1])
+        hid0 = lean(0, a_rows, idx3, [rows[:, 0:1] for rows in b_rows], "hid0")
+
+        hid1 = lean(1, b_rows, idx4, [rows[:, 0:1] for rows in a_rows[:-1]] + [la_last[:]], f"a_rows{PACK - 1}")
+        early = quantise(0, hid0)
+        short_way(1, "hid0", "woven")
+        p_early = product(0, *early)
+        late = quantise(1, hid1)
+
+        scatter(0, p_early)
+        scatter(1, product(1, *late))
+
+        for half in range(2):
+            total = tile(f"total{half}", [P, E], F32)
+            (nc.vector, nc.vector)[half].tensor_tensor(total[:], pages[half, 0][:], pages[half, 1][:], ADD)
+            nc.sync.dma_start(out[half * P:(half + 1) * P, :], total[:])

@@ -54,25 +54,15 @@ def tile_list_sidebyside_leaned_further_pagetwice_kernel(
         def fp8_rows(src):
             return src[0].rearrange("p n t -> p (n t)")
 
-        def zeroed_plane(name, cols):
+        def zeroed_plane(name, cols, engine=nc.vector):
             plane = tile(name, [P, cols], U8)
-            nc.vector.memset(plane[:].bitcast(I32), 0)
+            engine.memset(plane[:].bitcast(I32), 0)
             return plane
 
-        def load_plane(plane, src):
+        def load_plane(plane, src, queue=nc.sync):
             rows = src[0].bitcast(I32)
             for q in range(QUADS):
-                nc.sync.dma_start(plane[32 * q:32 * q + QROWS, :].bitcast(I32), rows[QROWS * q:QROWS * (q + 1), :])
-
-        def zeroed_fold(name, cols):
-            fold = tile(name, [P, QUADS, cols // 4], I32)
-            nc.vector.memset(fold[0:64, 0:QUADS:2, :], 0)
-            return fold
-
-        def load_fold(queue, fold, slot, src):
-            cols = src.shape[2] // 4
-            queue.dma_start(fold[0:QROWS, :, slot * cols:(slot + 1) * cols],
-                            src[0].bitcast(I32).rearrange("(q r) c -> r q c", r=QROWS))
+                queue.dma_start(plane[32 * q:32 * q + QROWS, :].bitcast(I32), rows[QROWS * q:QROWS * (q + 1), :])
 
         def load_pair(pair, slot, src):
             cols = src.shape[2] // 4
@@ -80,18 +70,13 @@ def tile_list_sidebyside_leaned_further_pagetwice_kernel(
             for odd in range(2):
                 nc.sync.dma_start(pair[32 * odd:32 * odd + QROWS, :, slot * cols:(slot + 1) * cols], rows[odd])
 
-        def unfold(fold):
-            nc.vector.tensor_copy(fold[32:32 + QROWS, 0:3, :], fold[0:QROWS, 1:4, :])
-            nc.vector.tensor_copy(fold[64:128, 0, :], fold[0:64, 2, :])
-            return fold[:, 0, :].bitcast(U8)
-
         def gather(name, window, entries, dtype, tag=None):
             picked = tile(name, [P, 16 * entries.shape[1]], dtype, tag)
             nc.vector.tensor_copy(picked[:], window[:].indirect(entries))
             return picked
 
         xt_plane = zeroed_plane("xt_plane", T)
-        w_fold = zeroed_fold("w_fold", R)
+        w_plane = zeroed_plane("w_plane", R)
         w20_pair = tile("w20_pair", [P, 2, 2 * R // 4], I32)
         nc.vector.memset(w20_pair[0:64], 0)
         xo_plane = zeroed_plane("xo_plane", Z)
@@ -100,13 +85,14 @@ def tile_list_sidebyside_leaned_further_pagetwice_kernel(
 
         idx = load_list("idx", offs)
         w_raw = load_words(nc.scalar, "w_raw", w_words[0], U16, R)
-        xt_tab = load_words(nc.sync, "xt_tab", fp8_rows(xt_words), U32, T)
-        load_fold(nc.scalar, w_fold, 0, w_scales)
+        w_stage = tile("w_stage", [QROWS, QUADS, R // 4], I32)
+        nc.sync.dma_start(w_stage[:], w_scales[0].bitcast(I32).rearrange("(q r) c -> r q c", r=QROWS))
         load_plane(xt_plane, xt_scales)
-        w2_raw = load_words(nc.sync, "w2_raw", fp8_rows(w2_words), U32, R)
+        xt_tab = load_words(nc.sync, "xt_tab", fp8_rows(xt_words), U32, T)
         load_pair(w20_pair, 0, w2_scales)
         load_pair(w20_pair, 1, w0_scales)
         idx2 = load_list("idx2", offs2)
+        w2_raw = load_words(nc.sync, "w2_raw", fp8_rows(w2_words), U32, R)
         xo_tab = load_words(nc.sync, "xo_tab", xo_words[0], U16, Z)
         w0_raw = load_words(nc.sync, "w0_raw", fp8_rows(w0_words), U32, R)
         load_plane(xo_plane, xo_scales)
@@ -127,10 +113,11 @@ def tile_list_sidebyside_leaned_further_pagetwice_kernel(
         w0_codes = tile("w0_codes", [P, R], U32)
         nc.scalar.copy(*dealt(w0_codes[:], w0_raw[:], LINE // 4))
 
+        for q in range(QUADS):
+            nc.vector.tensor_copy(w_plane[32 * q:32 * q + QROWS, :].bitcast(I32), w_stage[:, q, :])
         xg_scale = gather("xg_scale", xt_plane, idx[:], U8)
-        w_plane = unfold(w_fold)
         w_scale = tile("w_scale", [P, R], U8)
-        nc.vector.tensor_copy(*dealt(w_scale[:], w_plane, LINE))
+        nc.vector.tensor_copy(*dealt(w_scale[:], w_plane[:], LINE))
         xg_codes = gather("xg_codes", xt_tab, idx[:], U32)
         nc.vector.tensor_copy(w20_pair[64:128, 0, :], w20_pair[0:64, 1, :])
         w20_plane = w20_pair[:, 0, :].bitcast(U8)
@@ -168,6 +155,7 @@ def tile_list_sidebyside_leaned_further_pagetwice_kernel(
 
 
         p_acc = {}
+        p_rows = tile("p_rows", [P, 2, D], F32)
 
         def short_way(part, scale_tag, codes_tag):
             entries = idx5[:, part * HALF // 16:(part + 1) * HALF // 16]
@@ -186,7 +174,7 @@ def tile_list_sidebyside_leaned_further_pagetwice_kernel(
             return hid
 
         def quantise(part, hid):
-            woven = tile(f"woven{part}", [P, HALF, PACK], BF16, "woven")
+            woven = tile(f"woven{part}", [P, HALF, PACK], BF16)
             nc.vector.tensor_copy(woven[:].rearrange("p (c i) t -> p c t i", i=4),
                                   hid[:].rearrange("p t (c i) -> p c t i", i=4))
             hid_codes = tile(f"hid_codes{part}", [P, HALF], U32)
@@ -199,15 +187,10 @@ def tile_list_sidebyside_leaned_further_pagetwice_kernel(
                 cols = slice(half * P, (half + 1) * P)
                 nc.tensor.matmul_mx(p_acc[part][:, half, :], lhsT=wb_codes[:, cols].bitcast(E5M2), lhsT_scale=wb_plane[:, cols],
                                     rhs=hid_codes[:].bitcast(E4M3), rhs_scale=hid_scale[:], start=False, stop=half == 1)
-            p_rows = tile(f"p_rows{part}", [P, 2, HALF], F32)
-            nc.vector.tensor_copy(p_rows[:], p_acc[part][:])
-            return p_rows
+            (nc.scalar.copy, nc.vector.tensor_copy)[part](p_rows[:, :, part * HALF:(part + 1) * HALF], p_acc[part][:])
 
-        def scatter(part, p_rows):
-            entries = slice(part * HALF // 16, (part + 1) * HALF // 16)
-            for half in range(2):
-                nc.vector.tensor_copy(pages[half, 0][:].indirect(idx6[:, entries]), p_rows[:, half, :])
-                nc.scalar.activation(pages[half, 1][:].indirect(idx7[:, entries]), p_rows[:, half, :], COPY)
+        def scatter_b(half, lo, hi):
+            nc.scalar.activation(pages[half, 1][:].indirect(idx7[:, lo // 16:hi // 16]), p_rows[:, half, lo:hi], COPY)
 
         short_way(0, "og_scale", "og_codes")
         la_last = tile("la_last", [P, 1], F32)
@@ -216,14 +199,22 @@ def tile_list_sidebyside_leaned_further_pagetwice_kernel(
 
         hid1 = lean(1, b_rows, idx4, [rows[:, 0:1] for rows in a_rows[:-1]] + [la_last[:]], f"a_rows{PACK - 1}")
         early = quantise(0, hid0)
-        short_way(1, "hid0", "woven")
-        p_early = product(0, *early)
+        short_way(1, "hid0", "woven0")
+        product(0, *early)
         late = quantise(1, hid1)
 
-        scatter(0, p_early)
-        scatter(1, product(1, *late))
-
+        product(1, *late)
         for half in range(2):
-            total = tile(f"total{half}", [P, E], F32)
-            (nc.vector, nc.vector)[half].tensor_tensor(total[:], pages[half, 0][:], pages[half, 1][:], ADD)
-            nc.sync.dma_start(out[half * P:(half + 1) * P, :], total[:])
+            nc.vector.tensor_copy(pages[half, 0][:].indirect(idx6[:]), p_rows[:, half, :])
+        scatter_b(1, 0, HALF)
+        scatter_b(0, 0, D)
+        scatter_b(1, HALF, D)
+
+        first = tile("first", [P, E], F32)
+        nc.gpsimd.tensor_tensor(first[:], pages[0, 0][:], pages[0, 1][:], ADD)
+        nc.sync.dma_start(out[0:P, :], first[:])
+        for piece in range(2):
+            cols = slice(piece * E // 2, (piece + 1) * E // 2)
+            second = tile(f"second{piece}", [P, E // 2], F32)
+            nc.vector.tensor_tensor(second[:], pages[1, 0][:, cols], pages[1, 1][:, cols], ADD)
+            (nc.sync, nc.scalar)[piece].dma_start(out[P:2 * P, cols], second[:])

@@ -76,7 +76,7 @@ def tile_list_sidebyside_leaned_further_pagetwice_kernel(
             return picked
 
         xt_plane = zeroed_plane("xt_plane", T)
-        w_plane = zeroed_plane("w_plane", R)
+        w2_plane = zeroed_plane("w2_plane", R)
         w20_pair = tile("w20_pair", [P, 2, 2 * R // 4], I32)
         nc.vector.memset(w20_pair[0:64], 0)
         xo_plane = zeroed_plane("xo_plane", Z)
@@ -84,17 +84,17 @@ def tile_list_sidebyside_leaned_further_pagetwice_kernel(
         wb_plane = zeroed_plane("wb_plane", N)
 
         idx = load_list("idx", offs)
-        w_raw = load_words(nc.scalar, "w_raw", w_words[0], U16, R)
-        w_stage = tile("w_stage", [QROWS, QUADS, R // 4], I32)
-        nc.sync.dma_start(w_stage[:], w_scales[0].bitcast(I32).rearrange("(q r) c -> r q c", r=QROWS))
+        w2_raw = load_words(nc.scalar, "w2_raw", fp8_rows(w2_words), U32, R)
+        w2_stage = tile("w2_stage", [QROWS, QUADS, R // 4], I32)
+        nc.sync.dma_start(w2_stage[:], w2_scales[0].bitcast(I32).rearrange("(q r) c -> r q c", r=QROWS))
         load_plane(xt_plane, xt_scales)
         xt_tab = load_words(nc.sync, "xt_tab", fp8_rows(xt_words), U32, T)
-        load_pair(w20_pair, 0, w2_scales)
+        load_pair(w20_pair, 0, w_scales)
         load_pair(w20_pair, 1, w0_scales)
-        idx2 = load_list("idx2", offs2)
-        w2_raw = load_words(nc.sync, "w2_raw", fp8_rows(w2_words), U32, R)
-        xo_tab = load_words(nc.sync, "xo_tab", xo_words[0], U16, Z)
+        w_raw = load_words(nc.sync, "w_raw", w_words[0], U16, R)
         w0_raw = load_words(nc.sync, "w0_raw", fp8_rows(w0_words), U32, R)
+        xo_tab = load_words(nc.sync, "xo_tab", xo_words[0], U16, Z)
+        idx2 = load_list("idx2", offs2)
         load_plane(xo_plane, xo_scales)
         idx5 = load_list("idx5", offs5)
         idx3 = load_list("idx3", offs3)
@@ -106,34 +106,34 @@ def tile_list_sidebyside_leaned_further_pagetwice_kernel(
         idx6 = load_list("idx6", offs6)
         idx7 = load_list("idx7", offs7)
 
-        w_codes = tile("w_codes", [P, R], U16)
-        nc.scalar.copy(*dealt(w_codes[:], w_raw[:], LINE // 2))
         w2_codes = tile("w2_codes", [P, R], U32)
         nc.scalar.copy(*dealt(w2_codes[:], w2_raw[:], LINE // 4))
+        w_codes = tile("w_codes", [P, R], U16)
+        nc.scalar.copy(*dealt(w_codes[:], w_raw[:], LINE // 2))
         w0_codes = tile("w0_codes", [P, R], U32)
         nc.scalar.copy(*dealt(w0_codes[:], w0_raw[:], LINE // 4))
 
         for q in range(QUADS):
-            nc.vector.tensor_copy(w_plane[32 * q:32 * q + QROWS, :].bitcast(I32), w_stage[:, q, :])
+            nc.vector.tensor_copy(w2_plane[32 * q:32 * q + QROWS, :].bitcast(I32), w2_stage[:, q, :])
         xg_scale = gather("xg_scale", xt_plane, idx[:], U8)
-        w_scale = tile("w_scale", [P, R], U8)
-        nc.vector.tensor_copy(*dealt(w_scale[:], w_plane[:], LINE))
+        w2_scale = tile("w2_scale", [P, R], U8)
+        nc.vector.tensor_copy(*dealt(w2_scale[:], w2_plane[:], LINE))
         xg_codes = gather("xg_codes", xt_tab, idx[:], U32)
         nc.vector.tensor_copy(w20_pair[64:128, 0, :], w20_pair[0:64, 1, :])
         w20_plane = w20_pair[:, 0, :].bitcast(U8)
-        w2_scale = tile("w2_scale", [P, R], U8)
-        nc.vector.tensor_copy(*dealt(w2_scale[:], w20_plane[:, 0:R], LINE))
+        w_scale = tile("w_scale", [P, R], U8)
+        nc.vector.tensor_copy(*dealt(w_scale[:], w20_plane[:, 0:R], LINE))
         w0_scale = tile("w0_scale", [P, R], U8)
         nc.vector.tensor_copy(*dealt(w0_scale[:], w20_plane[:, R:2 * R], LINE))
         og_codes = gather("og_codes", xo_tab, idx2[:], U16)
         og_scale = gather("og_scale", xo_plane, idx2[:], U8)
 
-        pages = {}
-        for (half, which), tag in zip(((0, 0), (0, 1), (1, 0), (1, 1)), ("w_raw", "w2_raw", "w0_raw", "xo_tab")):
-            pages[half, which] = tile(f"page{half}{which}", [P, E], F32, tag)
-            nc.gpsimd.memset(pages[half, which][:], 0.0)
-
         a_rows, b_rows, b_acc = [], [], []
+        for t in range(PACK):
+            cols = slice(t * P, (t + 1) * P)
+            b_acc.append(psum.tile([P, J], F32, name=f"b_acc{t}", tag=f"bank{PACK + t}"))
+            nc.tensor.matmul_mx(b_acc[t][:], lhsT=w2_codes[:, cols].bitcast(E5M2), lhsT_scale=w2_scale[:, cols],
+                                rhs=xg_codes[:].bitcast(E4M3), rhs_scale=xg_scale[:], start=True, stop=False)
         for t in range(PACK):
             cols = slice(t * P, (t + 1) * P)
             acc = psum.tile([P, J], F32, name=f"a_acc{t}", tag=f"bank{t}")
@@ -143,15 +143,15 @@ def tile_list_sidebyside_leaned_further_pagetwice_kernel(
             nc.scalar.copy(a_rows[t][:], acc[:])
         for t in range(PACK):
             cols = slice(t * P, (t + 1) * P)
-            b_acc.append(psum.tile([P, J], F32, name=f"b_acc{t}", tag=f"bank{PACK + t}"))
-            nc.tensor.matmul_mx(b_acc[t][:], lhsT=w2_codes[:, cols].bitcast(E5M2), lhsT_scale=w2_scale[:, cols],
-                                rhs=xg_codes[:].bitcast(E4M3), rhs_scale=xg_scale[:], start=True, stop=False)
-        for t in range(PACK):
-            cols = slice(t * P, (t + 1) * P)
             nc.tensor.matmul_mx(b_acc[t][:], lhsT=w0_codes[:, cols].bitcast(E5M2), lhsT_scale=w0_scale[:, cols],
                                 rhs=og_codes[:].bitcast(E2M1), rhs_scale=og_scale[:], start=False, stop=True)
             b_rows.append(tile(f"b_rows{t}", [P, J], F32))
             nc.vector.tensor_copy(b_rows[t][:], b_acc[t][:])
+
+        pages = {}
+        for (half, which), tag in zip(((0, 0), (0, 1), (1, 0), (1, 1)), ("xo_plane", "xg_codes", "w_codes", "w0_codes")):
+            pages[half, which] = tile(f"page{half}{which}", [P, E], F32, tag)
+            nc.gpsimd.memset(pages[half, which][:], 0.0)
 
 
         p_acc = {}

@@ -23,6 +23,7 @@ QUADS = 4
 QROWS = 4
 HALF = D // 2
 LINE = 16
+SHARE = 64
 
 
 def dealt(dst, src, run):
@@ -189,8 +190,12 @@ def tile_list_sidebyside_leaned_further_pagetwice_kernel(
                                     rhs=hid_codes[:].bitcast(E4M3), rhs_scale=hid_scale[:], start=False, stop=half == 1)
             (nc.scalar.copy, nc.vector.tensor_copy)[part](p_rows[:, :, part * HALF:(part + 1) * HALF], p_acc[part][:])
 
-        def scatter_b(half, lo, hi):
-            nc.scalar.activation(pages[half, 1][:].indirect(idx7[:, lo // 16:hi // 16]), p_rows[:, half, lo:hi], COPY)
+        def scatter(on_vector, half, which, lo, hi):
+            window = pages[half, which][:].indirect((idx6, idx7)[which][:, lo // 16:hi // 16])
+            if on_vector:
+                nc.vector.tensor_copy(window, p_rows[:, half, lo:hi])
+            else:
+                nc.scalar.activation(window, p_rows[:, half, lo:hi], COPY)
 
         short_way(0, "og_scale", "og_codes")
         la_last = tile("la_last", [P, 1], F32)
@@ -204,14 +209,15 @@ def tile_list_sidebyside_leaned_further_pagetwice_kernel(
         late = quantise(1, hid1)
 
         product(1, *late)
-        for half in range(2):
-            nc.vector.tensor_copy(pages[half, 0][:].indirect(idx6[:]), p_rows[:, half, :])
-        scatter_b(1, 0, HALF)
-        scatter_b(0, 0, D)
-        scatter_b(1, HALF, D)
+        scatter(True, 0, 0, 0, D)
+        scatter(True, 1, 0, 0, D - SHARE)
+        scatter(False, 1, 1, 0, HALF)
+        scatter(False, 0, 1, 0, D)
+        scatter(False, 1, 1, HALF, D)
+        scatter(False, 1, 0, D - SHARE, D)
 
         first = tile("first", [P, E], F32)
-        nc.gpsimd.tensor_tensor(first[:], pages[0, 0][:], pages[0, 1][:], ADD)
+        nc.vector.tensor_tensor(first[:], pages[0, 0][:], pages[0, 1][:], ADD)
         nc.sync.dma_start(out[0:P, :], first[:])
         for piece in range(2):
             cols = slice(piece * E // 2, (piece + 1) * E // 2)

from contextlib import ExitStack

import concourse.mybir as mybir

K, T, J, R, F, Z, O, U, D, N, E = 512, 1024, 256, 512, 512, 1024, 128, 128, 256, 256, 512
FLOPS = 2 * (K * R * J + K * R * J + F * R * J + R * N * D + K * N * D)

F32 = mybir.dt.float32
BF16 = mybir.dt.bfloat16
I32 = mybir.dt.int32
U32 = mybir.dt.uint32
U16 = mybir.dt.uint16
U8 = mybir.dt.uint8
E4M3 = mybir.dt.float8_e4m3fn_x4
E5M2 = mybir.dt.float8_e5m2_x4
E2M1 = mybir.dt.float4_e2m1fn_x4
COPY = mybir.ActivationFunctionType.Copy
ADD = mybir.AluOpType.add

P = 128
PACK = 4
QUADS = 4
QROWS = 4
HALF = D // 2
LINE = 16
SHARE = 64


def dealt(dst, src, run):
    return (dst.rearrange("p (t c i) -> p c t i", t=PACK, i=run),
            src.rearrange("p (c i t) -> p c t i", t=PACK, i=run))


def tile_list_sidebyside_leaned_further_pagetwice_kernel(
        tc, xt_words, xt_scales, xo_words, xo_scales, w_words, w_scales, w2_words, w2_scales, w0_words, w0_scales,
        wb_words, wb_scales, ws_words, ws_scales, offs, offs2, offs3, offs4, offs5, offs6, offs7, out):
    nc = tc.nc
    with ExitStack() as ctx:
        sb = ctx.enter_context(tc.tile_pool(name="sb", bufs=1))
        psum = ctx.enter_context(tc.psum_pool(name="psum", bufs=1))

        def tile(name, shape, dtype, tag=None):
            return sb.tile(shape, dtype, name=name, tag=tag or name, align_bytes=64)

        def load_list(name, src):
            lst = sb.tile(list(src.shape), U16, name=name)
            nc.sync.dma_start(lst[:], src)
            return lst

        def load_words(queue, name, src, dtype, cols):
            words = tile(name, [P, cols], dtype)
            queue.dma_start(words[:].bitcast(I32), src.bitcast(I32))
            return words

        def fp8_rows(src):
            return src[0].rearrange("p n t -> p (n t)")

        def zeroed_plane(name, cols, engine=nc.vector):
            plane = tile(name, [P, cols], U8)
            engine.memset(plane[:].bitcast(I32), 0)
            return plane

        def load_plane(plane, src, queue=nc.sync):
            rows = src[0].bitcast(I32)
            for q in range(QUADS):
                queue.dma_start(plane[32 * q:32 * q + QROWS, :].bitcast(I32), rows[QROWS * q:QROWS * (q + 1), :])

        def load_pair(pair, slot, src):
            cols = src.shape[2] // 4
            rows = src[0].bitcast(I32).rearrange("(high odd r) c -> odd r high c", odd=2, r=QROWS)
            for odd in range(2):
                nc.sync.dma_start(pair[32 * odd:32 * odd + QROWS, :, slot * cols:(slot + 1) * cols], rows[odd])

        def gather(name, window, entries, dtype, tag=None):
            picked = tile(name, [P, 16 * entries.shape[1]], dtype, tag)
            nc.vector.tensor_copy(picked[:], window[:].indirect(entries))
            return picked

        xt_plane = zeroed_plane("xt_plane", T)
        w2_plane = zeroed_plane("w2_plane", R)
        w20_pair = tile("w20_pair", [P, 2, 2 * R // 4], I32)
        nc.vector.memset(w20_pair[0:64], 0)
        xo_plane = zeroed_plane("xo_plane", Z)
        ws_plane = zeroed_plane("ws_plane", N)
        wb_plane = zeroed_plane("wb_plane", N)

        idx = load_list("idx", offs)
        w2_raw = load_words(nc.scalar, "w2_raw", fp8_rows(w2_words), U32, R)
        w2_stage = tile("w2_stage", [QROWS, QUADS, R // 4], I32)
        nc.sync.dma_start(w2_stage[:], w2_scales[0].bitcast(I32).rearrange("(q r) c -> r q c", r=QROWS))
        load_plane(xt_plane, xt_scales)
        xt_tab = load_words(nc.sync, "xt_tab", fp8_rows(xt_words), U32, T)
        load_pair(w20_pair, 0, w_scales)
        load_pair(w20_pair, 1, w0_scales)
        w_raw = load_words(nc.sync, "w_raw", w_words[0], U16, R)
        w0_raw = load_words(nc.sync, "w0_raw", fp8_rows(w0_words), U32, R)
        xo_tab = load_words(nc.sync, "xo_tab", xo_words[0], U16, Z)
        idx2 = load_list("idx2", offs2)
        load_plane(xo_plane, xo_scales)
        idx5 = load_list("idx5", offs5)
        idx3 = load_list("idx3", offs3)
        idx4 = load_list("idx4", offs4)
        ws_codes = load_words(nc.sync, "ws_codes", fp8_rows(ws_words), U32, N)
        load_plane(ws_plane, ws_scales)
        wb_codes = load_words(nc.sync, "wb_codes", fp8_rows(wb_words), U32, N)
        load_plane(wb_plane, wb_scales)
        idx6 = load_list("idx6", offs6)
        idx7 = load_list("idx7", offs7)

        w2_codes = tile("w2_codes", [P, R], U32)
        nc.scalar.copy(*dealt(w2_codes[:], w2_raw[:], LINE // 4))
        w_codes = tile("w_codes", [P, R], U16)
        nc.scalar.copy(*dealt(w_codes[:], w_raw[:], LINE // 2))
        w0_codes = tile("w0_codes", [P, R], U32)
        nc.scalar.copy(*dealt(w0_codes[:], w0_raw[:], LINE // 4))

        for q in range(QUADS):
            nc.vector.tensor_copy(w2_plane[32 * q:32 * q + QROWS, :].bitcast(I32), w2_stage[:, q, :])
        xg_scale = gather("xg_scale", xt_plane, idx[:], U8)
        w2_scale = tile("w2_scale", [P, R], U8)
        nc.vector.tensor_copy(*dealt(w2_scale[:], w2_plane[:], LINE))
        xg_codes = gather("xg_codes", xt_tab, idx[:], U32)
        nc.vector.tensor_copy(w20_pair[64:128, 0, :], w20_pair[0:64, 1, :])
        w20_plane = w20_pair[:, 0, :].bitcast(U8)
        w_scale = tile("w_scale", [P, R], U8)
        nc.vector.tensor_copy(*dealt(w_scale[:], w20_plane[:, 0:R], LINE))
        w0_scale = tile("w0_scale", [P, R], U8)
        nc.vector.tensor_copy(*dealt(w0_scale[:], w20_plane[:, R:2 * R], LINE))
        og_codes = gather("og_codes", xo_tab, idx2[:], U16)
        og_scale = gather("og_scale", xo_plane, idx2[:], U8)

        a_rows, b_rows, b_acc = [], [], []
        for t in range(PACK):
            cols = slice(t * P, (t + 1) * P)
            b_acc.append(psum.tile([P, J], F32, name=f"b_acc{t}", tag=f"bank{PACK + t}"))
            nc.tensor.matmul_mx(b_acc[t][:], lhsT=w2_codes[:, cols].bitcast(E5M2), lhsT_scale=w2_scale[:, cols],
                                rhs=xg_codes[:].bitcast(E4M3), rhs_scale=xg_scale[:], start=True, stop=False)
        for t in range(PACK):
            cols = slice(t * P, (t + 1) * P)
            acc = psum.tile([P, J], F32, name=f"a_acc{t}", tag=f"bank{t}")
            nc.tensor.matmul_mx(acc[:], lhsT=w_codes[:, cols].bitcast(E2M1), lhsT_scale=w_scale[:, cols],
                                rhs=xg_codes[:].bitcast(E4M3), rhs_scale=xg_scale[:], start=True, stop=True)
            a_rows.append(tile(f"a_rows{t}", [P, J], F32))
            nc.scalar.copy(a_rows[t][:], acc[:])
        for t in range(PACK):
            cols = slice(t * P, (t + 1) * P)
            nc.tensor.matmul_mx(b_acc[t][:], lhsT=w0_codes[:, cols].bitcast(E5M2), lhsT_scale=w0_scale[:, cols],
                                rhs=og_codes[:].bitcast(E2M1), rhs_scale=og_scale[:], start=False, stop=True)
            b_rows.append(tile(f"b_rows{t}", [P, J], F32))
            nc.vector.tensor_copy(b_rows[t][:], b_acc[t][:])

        pages = {}
        for (half, which), tag in zip(((0, 0), (0, 1), (1, 0), (1, 1)), ("xo_plane", "xg_codes", "w_codes", "w0_codes")):
            pages[half, which] = tile(f"page{half}{which}", [P, E], F32, tag)
            nc.gpsimd.memset(pages[half, which][:], 0.0)


        p_acc = {}
        p_rows = tile("p_rows", [P, 2, D], F32)

        def short_way(part, scale_tag, codes_tag):
            entries = idx5[:, part * HALF // 16:(part + 1) * HALF // 16]
            sg_scale = gather(f"sg_scale{part}", xt_plane, entries, U8, scale_tag)
            sg_codes = gather(f"sg_codes{part}", xt_tab, entries, U32, codes_tag)
            p_acc[part] = psum.tile([P, 2, HALF], F32, name=f"p_acc{part}", tag=f"bank{part}")
            for half in range(2):
                cols = slice(half * P, (half + 1) * P)
                nc.tensor.matmul_mx(p_acc[part][:, half, :], lhsT=ws_codes[:, cols].bitcast(E5M2), lhsT_scale=ws_plane[:, cols],
                                    rhs=sg_codes[:].bitcast(E4M3), rhs_scale=sg_scale[:], start=half == 0, stop=False)

        def lean(part, rows, lst, scales, tag):
            hid = tile(f"hid{part}", [P, PACK, HALF], BF16, tag)
            for t in range(PACK):
                nc.scalar.activation(hid[:, t, :], rows[t][:].indirect(lst[:]), COPY, scale=scales[t])
            return hid

        def quantise(part, hid):
            woven = tile(f"woven{part}", [P, HALF, PACK], BF16)
            nc.vector.tensor_copy(woven[:].rearrange("p (c i) t -> p c t i", i=4),
                                  hid[:].rearrange("p t (c i) -> p c t i", i=4))
            hid_codes = tile(f"hid_codes{part}", [P, HALF], U32)
            hid_scale = tile(f"hid_scale{part}", [P, HALF], U8)
            nc.vector.quantize_mx(hid_codes[:].bitcast(E4M3), hid_scale[:], woven[:].rearrange("p d t -> p (d t)"))
            return hid_codes, hid_scale

        def product(part, hid_codes, hid_scale):
            for half in range(2):
                cols = slice(half * P, (half + 1) * P)
                nc.tensor.matmul_mx(p_acc[part][:, half, :], lhsT=wb_codes[:, cols].bitcast(E5M2), lhsT_scale=wb_plane[:, cols],
                                    rhs=hid_codes[:].bitcast(E4M3), rhs_scale=hid_scale[:], start=False, stop=half == 1)
            (nc.scalar.copy, nc.vector.tensor_copy)[part](p_rows[:, :, part * HALF:(part + 1) * HALF], p_acc[part][:])

        def scatter(on_vector, half, which, lo, hi):
            window = pages[half, which][:].indirect((idx6, idx7)[which][:, lo // 16:hi // 16])
            if on_vector:
                nc.vector.tensor_copy(window, p_rows[:, half, lo:hi])
            else:
                nc.scalar.activation(window, p_rows[:, half, lo:hi], COPY)

        short_way(0, "og_scale", "og_codes")
        la_last = tile("la_last", [P, 1], F32)
        nc.scalar.copy(la_last[:], a_rows[PACK - 1][:, 0:1])
        hid0 = lean(0, a_rows, idx3, [rows[:, 0:1] for rows in b_rows], "hid0")

        hid1 = lean(1, b_rows, idx4, [rows[:, 0:1] for rows in a_rows[:-1]] + [la_last[:]], f"a_rows{PACK - 1}")
        early = quantise(0, hid0)
        short_way(1, "hid0", "woven0")
        product(0, *early)
        late = quantise(1, hid1)

        product(1, *late)
        scatter(True, 0, 0, 0, D)
        scatter(True, 1, 0, 0, D - SHARE)
        scatter(False, 1, 1, 0, HALF)
        scatter(False, 0, 1, 0, D)
        scatter(False, 1, 1, HALF, D)
        scatter(False, 1, 0, D - SHARE, D)

        first = tile("first", [P, E], F32)
        nc.vector.tensor_tensor(first[:], pages[0, 0][:], pages[0, 1][:], ADD)
        nc.sync.dma_start(out[0:P, :], first[:])
        for piece in range(2):
            cols = slice(piece * E // 2, (piece + 1) * E // 2)
            second = tile(f"second{piece}", [P, E // 2], F32)
            nc.vector.tensor_tensor(second[:], pages[1, 0][:, cols], pages[1, 1][:, cols], ADD)
            (nc.sync, nc.scalar)[piece].dma_start(out[P:2 * P, cols], second[:])
